import numpy as np
import ml_dtypes

BF16 = ml_dtypes.bfloat16


def bf(x):
    return np.asarray(x, np.float32).astype(BF16)


def f32(x):
    return np.asarray(x, np.float32)


def f64(x):
    return np.asarray(x).astype(np.float64)


def striped(idx):
    return np.tile(idx.reshape(-1, 16).T, (8, 1))


def rows(idx, k):
    return np.tile(idx, (k, 1))


def look(tab, idx):
    return np.take_along_axis(f64(tab), rows(idx, len(tab)), axis=1)


K, S, H, D, V, N, M = 128, 2048, 256, 3, 512, 1536, 512


def setup_inputs():
    return {"z": bf(np.random.standard_normal((H, S))), "wt": bf(np.random.standard_normal((H, K)) / np.sqrt(H)), "u0": f32(np.random.uniform(0.2, 1.0, (K, V))), "u1": f32(np.random.uniform(0.2, 1.0, (K, V))), "u2": f32(np.random.uniform(0.2, 1.0, (K, V))), "w": bf(np.random.standard_normal((K, M)) / np.sqrt(K)), "b": f32(0.5 * np.random.standard_normal((M, 1))), "offs": striped(np.random.permutation(S)[:N])}


def reference(z, wt, u0, u1, u2, w, b, offs):
    idx = offs[:16].T.reshape(-1)
    tab = f64(wt).T @ f64(z)
    x = f64(u0) * look(tab, idx[:V]) + f64(u1) * look(tab, idx[1 * V:2 * V]) + f64(u2) * look(tab, idx[2 * V:3 * V])
    return np.maximum(f64(w).T @ x + f64(b), 0.0)

@@ -1,0 +1,82 @@
+import concourse.mybir as mybir
+
+BF16, F32, U16 = mybir.dt.bfloat16, mybir.dt.float32, mybir.dt.uint16
+MULT, ADD, MAX = mybir.AluOpType.mult, mybir.AluOpType.add, mybir.AluOpType.max
+RELU = mybir.ActivationFunctionType.Relu
+
+P = 128
+H, S = 256, 2048
+D, V = 3, 512
+M = 512
+KH = H // P
+MB = M // P
+Z_COLS = 512
+T_COLS = 256
+LIST_COLS = V // 16
+
+FLOPS = 2 * P * H * S + (2 * D - 1) * P * V + 2 * P * M * V + 2 * M * V
+
+
+def tile_lookup_pjmix_relu_kernel(tc, z, wt, u0, u1, u2, w, b, offs, out):
+    nc = tc.nc
+    with (
+        tc.tile_pool(name="held", bufs=1) as held,
+        tc.psum_pool(name="psum", bufs=8) as psum,
+    ):
+        wt_sb = held.tile([P, KH, P], BF16)
+        nc.sync.dma_start(wt_sb[:], wt.rearrange("(p h) r -> p h r", h=KH))
+        z_rows = z.rearrange("(p h) i -> p h i", h=KH)
+        z_tiles = []
+        for c in range(S // Z_COLS):
+            z_sb = held.tile([P, KH, Z_COLS], BF16, name=f"z_sb{c}")
+            nc.sync.dma_start(z_sb[:], z_rows[:, :, c * Z_COLS : (c + 1) * Z_COLS])
+            z_tiles.append(z_sb)
+        offsets = held.tile([P, D * LIST_COLS], U16)
+        nc.sync.dma_start(offsets[:], offs)
+        u_tiles = []
+        for d, u in enumerate((u0, u1, u2)):
+            u_sb = held.tile([P, V], F32, name=f"u_sb{d}")
+            nc.sync.dma_start(u_sb[:], u)
+            u_tiles.append(u_sb)
+        w_sb = held.tile([P, M], BF16)
+        nc.sync.dma_start(w_sb[:], w)
+        b_sb = held.tile([P, MB], F32)
+        nc.sync.dma_start(b_sb[:], b.rearrange("(p c) o -> p (c o)", c=MB))
+
+        table = held.tile([P, S], F32)
+        for t in range(S // T_COLS):
+            z_sb = z_tiles[t * T_COLS // Z_COLS]
+            first = t * T_COLS % Z_COLS
+            projected = psum.tile([P, T_COLS], F32, name="bank")
+            for h in range(KH):
+                nc.tensor.matmul(
+                    projected[:], wt_sb[:, h, :], z_sb[:, h, first : first + T_COLS], start=h == 0, stop=h == KH - 1
+                )
+            columns = table[:, t * T_COLS : (t + 1) * T_COLS]
+            if t % 2 == 0:
+                nc.scalar.copy(columns, projected[:])
+            else:
+                nc.vector.tensor_copy(columns, projected[:])
+
+        products = []
+        for d in range(D):
+            product = held.tile([P, V], F32, name=f"product{d}")
+            looked_up = table[:].indirect(offsets[:, d * LIST_COLS : (d + 1) * LIST_COLS])
+            nc.vector.tensor_tensor(product[:], looked_up, u_tiles[d][:], MULT)
+            products.append(product)
+        partial = held.tile([P, V], F32)
+        nc.vector.tensor_tensor(partial[:], products[0][:], products[1][:], ADD)
+        x_sb = held.tile([P, V], BF16)
+        nc.vector.tensor_tensor(x_sb[:], partial[:], products[2][:], ADD)
+
+        w_blocks = w_sb[:].rearrange("r (p c) -> r c p", c=MB)
+        out_rows = out.rearrange("(p c) j -> p c j", c=MB)
+        for c in range(MB):
+            layer = psum.tile([P, V], F32, name="bank")
+            nc.tensor.matmul(layer[:], w_blocks[:, c, :], x_sb[:], start=True, stop=True)
+            y_sb = held.tile([P, V], F32, name=f"y_sb{c}")
+            if c % 2 == 0:
+                nc.scalar.activation(y_sb[:], layer[:], RELU, bias=b_sb[:, c : c + 1])
+            else:
+                nc.vector.tensor_scalar(y_sb[:], layer[:], b_sb[:, c : c + 1], 0.0, ADD, MAX)
+            nc.sync.dma_start(out_rows[:, c, :], y_sb[:])

@@ -12,7 +12,7 @@ KH = H // P
 MB = M // P
 Z_COLS = 512
 T_COLS = 256
-LIST_COLS = V // 16
+X_COLS = 256
 
 FLOPS = 2 * P * H * S + (2 * D - 1) * P * V + 2 * P * M * V + 2 * M * V
 
@@ -21,6 +21,7 @@ def tile_lookup_pjmix_relu_kernel(tc, z, wt, u0, u1, u2, w, b, offs, out):
     nc = tc.nc
     with (
         tc.tile_pool(name="held", bufs=1) as held,
+        tc.tile_pool(name="work", bufs=2) as work,
         tc.psum_pool(name="psum", bufs=8) as psum,
     ):
         wt_sb = held.tile([P, KH, P], BF16)
@@ -31,7 +32,7 @@ def tile_lookup_pjmix_relu_kernel(tc, z, wt, u0, u1, u2, w, b, offs, out):
             z_sb = held.tile([P, KH, Z_COLS], BF16, name=f"z_sb{c}")
             nc.sync.dma_start(z_sb[:], z_rows[:, :, c * Z_COLS : (c + 1) * Z_COLS])
             z_tiles.append(z_sb)
-        offsets = held.tile([P, D * LIST_COLS], U16)
+        offsets = held.tile([P, D * V // 16], U16)
         nc.sync.dma_start(offsets[:], offs)
         u_tiles = []
         for d, u in enumerate((u0, u1, u2)):
@@ -58,25 +59,27 @@ def tile_lookup_pjmix_relu_kernel(tc, z, wt, u0, u1, u2, w, b, offs, out):
             else:
                 nc.vector.tensor_copy(columns, projected[:])
 
-        products = []
-        for d in range(D):
-            product = held.tile([P, V], F32, name=f"product{d}")
-            looked_up = table[:].indirect(offsets[:, d * LIST_COLS : (d + 1) * LIST_COLS])
-            nc.vector.tensor_tensor(product[:], looked_up, u_tiles[d][:], MULT)
-            products.append(product)
-        partial = held.tile([P, V], F32)
-        nc.vector.tensor_tensor(partial[:], products[0][:], products[1][:], ADD)
-        x_sb = held.tile([P, V], BF16)
-        nc.vector.tensor_tensor(x_sb[:], partial[:], products[2][:], ADD)
-
         w_blocks = w_sb[:].rearrange("r (p c) -> r c p", c=MB)
         out_rows = out.rearrange("(p c) j -> p c j", c=MB)
-        for c in range(MB):
-            layer = psum.tile([P, V], F32, name="bank")
-            nc.tensor.matmul(layer[:], w_blocks[:, c, :], x_sb[:], start=True, stop=True)
-            y_sb = held.tile([P, V], F32, name=f"y_sb{c}")
-            if c % 2 == 0:
-                nc.scalar.activation(y_sb[:], layer[:], RELU, bias=b_sb[:, c : c + 1])
-            else:
-                nc.vector.tensor_scalar(y_sb[:], layer[:], b_sb[:, c : c + 1], 0.0, ADD, MAX)
-            nc.sync.dma_start(out_rows[:, c, :], y_sb[:])
+        for first in range(0, V, X_COLS):
+            products = []
+            for d in range(D):
+                product = work.tile([P, X_COLS], F32, name=f"product{d}")
+                entry = d * V + first
+                looked_up = table[:].indirect(offsets[:, entry // 16 : (entry + X_COLS) // 16])
+                nc.vector.tensor_tensor(product[:], looked_up, u_tiles[d][:, first : first + X_COLS], MULT)
+                products.append(product)
+            partial = work.tile([P, X_COLS], F32)
+            nc.vector.tensor_tensor(partial[:], products[0][:], products[1][:], ADD)
+            x_sb = work.tile([P, X_COLS], BF16)
+            nc.vector.tensor_tensor(x_sb[:], partial[:], products[2][:], ADD)
+
+            for c in range(MB):
+                layer = psum.tile([P, X_COLS], F32, name="bank")
+                nc.tensor.matmul(layer[:], w_blocks[:, c, :], x_sb[:], start=True, stop=True)
+                y_sb = work.tile([P, X_COLS], F32, name=f"y_sb{c}")
+                if c % 2 == 0:
+                    nc.scalar.activation(y_sb[:], layer[:], RELU, bias=b_sb[:, c : c + 1])
+                else:
+                    nc.vector.tensor_scalar(y_sb[:], layer[:], b_sb[:, c : c + 1], 0.0, ADD, MAX)
+                nc.sync.dma_start(out_rows[:, c, first : first + X_COLS], y_sb[:])

@@ -13,6 +13,7 @@ MB = M // P
 Z_COLS = 512
 T_COLS = 256
 X_COLS = 256
+WARM_COLS, WARM_UPS = 512, 6
 
 FLOPS = 2 * P * H * S + (2 * D - 1) * P * V + 2 * P * M * V + 2 * M * V
 
@@ -24,6 +25,12 @@ def tile_lookup_pjmix_relu_kernel(tc, z, wt, u0, u1, u2, w, b, offs, out):
         tc.tile_pool(name="work", bufs=2) as work,
         tc.psum_pool(name="psum", bufs=8) as psum,
     ):
+        zeros = held.tile([P, WARM_COLS], BF16)
+        nc.vector.memset(zeros[:], 0.0)
+        warm = psum.tile([P, WARM_COLS], F32, name="bank")
+        for step in range(WARM_UPS):
+            nc.tensor.matmul(warm[:], zeros[:, :P], zeros[:], start=True, stop=True)
+
         wt_sb = held.tile([P, KH, P], BF16)
         nc.sync.dma_start(wt_sb[:], wt.rearrange("(p h) r -> p h r", h=KH))
         z_rows = z.rearrange("(p h) i -> p h i", h=KH)
@@ -37,12 +44,12 @@ def tile_lookup_pjmix_relu_kernel(tc, z, wt, u0, u1, u2, w, b, offs, out):
         u_tiles = []
         for d, u in enumerate((u0, u1, u2)):
             u_sb = held.tile([P, V], F32, name=f"u_sb{d}")
-            nc.sync.dma_start(u_sb[:], u)
+            nc.gpsimd.dma_start(u_sb[:], u)
             u_tiles.append(u_sb)
         w_sb = held.tile([P, M], BF16)
-        nc.sync.dma_start(w_sb[:], w)
+        nc.gpsimd.dma_start(w_sb[:], w)
         b_sb = held.tile([P, MB], F32)
-        nc.sync.dma_start(b_sb[:], b.rearrange("(p c) o -> p (c o)", c=MB))
+        nc.gpsimd.dma_start(b_sb[:], b.rearrange("(p c) o -> p (c o)", c=MB))
 
         table = held.tile([P, S], F32)
         for t in range(S // T_COLS):
@@ -61,25 +68,34 @@ def tile_lookup_pjmix_relu_kernel(tc, z, wt, u0, u1, u2, w, b, offs, out):
 
         w_blocks = w_sb[:].rearrange("r (p c) -> r c p", c=MB)
         out_rows = out.rearrange("(p c) j -> p c j", c=MB)
-        for first in range(0, V, X_COLS):
-            products = []
-            for d in range(D):
-                product = work.tile([P, X_COLS], F32, name=f"product{d}")
-                entry = d * V + first
-                looked_up = table[:].indirect(offsets[:, entry // 16 : (entry + X_COLS) // 16])
-                nc.vector.tensor_tensor(product[:], looked_up, u_tiles[d][:, first : first + X_COLS], MULT)
-                products.append(product)
-            partial = work.tile([P, X_COLS], F32)
-            nc.vector.tensor_tensor(partial[:], products[0][:], products[1][:], ADD)
-            x_sb = work.tile([P, X_COLS], BF16)
-            nc.vector.tensor_tensor(x_sb[:], partial[:], products[2][:], ADD)
 
+        def look_up(first, d):
+            product = work.tile([P, X_COLS], F32, name=f"product{d}")
+            entry = d * V + first
+            looked_up = table[:].indirect(offsets[:, entry // 16 : (entry + X_COLS) // 16])
+            nc.vector.tensor_tensor(product[:], looked_up, u_tiles[d][:, first : first + X_COLS], MULT)
+            return product
+
+        def add(a, b, dtype, name):
+            total = work.tile([P, X_COLS], dtype, name=name)
+            nc.vector.tensor_tensor(total[:], a[:], b[:], ADD)
+            return total
+
+        def dense_layer(first, x_sb, vector_is_free):
             for c in range(MB):
                 layer = psum.tile([P, X_COLS], F32, name="bank")
                 nc.tensor.matmul(layer[:], w_blocks[:, c, :], x_sb[:], start=True, stop=True)
                 y_sb = work.tile([P, X_COLS], F32, name=f"y_sb{c}")
-                if c % 2 == 0:
+                if c % 2 == 0 or not vector_is_free:
                     nc.scalar.activation(y_sb[:], layer[:], RELU, bias=b_sb[:, c : c + 1])
                 else:
                     nc.vector.tensor_scalar(y_sb[:], layer[:], b_sb[:, c : c + 1], 0.0, ADD, MAX)
                 nc.sync.dma_start(out_rows[:, c, first : first + X_COLS], y_sb[:])
+
+        left0, left1, left2 = look_up(0, 0), look_up(0, 1), look_up(0, 2)
+        left01 = add(left0, left1, F32, "partial")
+        right0, right1 = look_up(X_COLS, 0), look_up(X_COLS, 1)
+        dense_layer(0, add(left01, left2, BF16, "x_sb"), vector_is_free=False)
+        right01 = add(right0, right1, F32, "partial")
+        right2 = look_up(X_COLS, 2)
+        dense_layer(X_COLS, add(right01, right2, BF16, "x_sb"), vector_is_free=True)

@@ -13,7 +13,7 @@ MB = M // P
 Z_COLS = 512
 T_COLS = 256
 X_COLS = 256
-WARM_COLS, WARM_UPS = 512, 6
+WARM_COLS, WARM_UPS = 512, 3
 
 FLOPS = 2 * P * H * S + (2 * D - 1) * P * V + 2 * P * M * V + 2 * M * V
 
@@ -47,9 +47,9 @@ def tile_lookup_pjmix_relu_kernel(tc, z, wt, u0, u1, u2, w, b, offs, out):
             nc.gpsimd.dma_start(u_sb[:], u)
             u_tiles.append(u_sb)
         w_sb = held.tile([P, M], BF16)
-        nc.gpsimd.dma_start(w_sb[:], w)
+        nc.sync.dma_start(w_sb[:], w)
         b_sb = held.tile([P, MB], F32)
-        nc.gpsimd.dma_start(b_sb[:], b.rearrange("(p c) o -> p (c o)", c=MB))
+        nc.sync.dma_start(b_sb[:], b.rearrange("(p c) o -> p (c o)", c=MB))
 
         table = held.tile([P, S], F32)
         for t in range(S // T_COLS):
@@ -94,8 +94,8 @@ def tile_lookup_pjmix_relu_kernel(tc, z, wt, u0, u1, u2, w, b, offs, out):
 
         left0, left1, left2 = look_up(0, 0), look_up(0, 1), look_up(0, 2)
         left01 = add(left0, left1, F32, "partial")
-        right0, right1 = look_up(X_COLS, 0), look_up(X_COLS, 1)
+        right0 = look_up(X_COLS, 0)
         dense_layer(0, add(left01, left2, BF16, "x_sb"), vector_is_free=False)
+        right1, right2 = look_up(X_COLS, 1), look_up(X_COLS, 2)
         right01 = add(right0, right1, F32, "partial")
-        right2 = look_up(X_COLS, 2)
         dense_layer(X_COLS, add(right01, right2, BF16, "x_sb"), vector_is_free=True)

import concourse.mybir as mybir

BF16, F32, U16 = mybir.dt.bfloat16, mybir.dt.float32, mybir.dt.uint16
MULT, ADD, MAX = mybir.AluOpType.mult, mybir.AluOpType.add, mybir.AluOpType.max
RELU = mybir.ActivationFunctionType.Relu

P = 128
H, S = 256, 2048
D, V = 3, 512
M = 512
KH = H // P
MB = M // P
Z_COLS = 512
T_COLS = 256
X_COLS = 256
WARM_COLS, WARM_UPS = 512, 3

FLOPS = 2 * P * H * S + (2 * D - 1) * P * V + 2 * P * M * V + 2 * M * V


def tile_lookup_pjmix_relu_kernel(tc, z, wt, u0, u1, u2, w, b, offs, out):
    nc = tc.nc
    with (
        tc.tile_pool(name="held", bufs=1) as held,
        tc.tile_pool(name="work", bufs=2) as work,
        tc.psum_pool(name="psum", bufs=8) as psum,
    ):
        zeros = held.tile([P, WARM_COLS], BF16)
        nc.vector.memset(zeros[:], 0.0)
        warm = psum.tile([P, WARM_COLS], F32, name="bank")
        for step in range(WARM_UPS):
            nc.tensor.matmul(warm[:], zeros[:, :P], zeros[:], start=True, stop=True)

        wt_sb = held.tile([P, KH, P], BF16)
        nc.sync.dma_start(wt_sb[:], wt.rearrange("(p h) r -> p h r", h=KH))
        z_rows = z.rearrange("(p h) i -> p h i", h=KH)
        z_tiles = []
        for c in range(S // Z_COLS):
            z_sb = held.tile([P, KH, Z_COLS], BF16, name=f"z_sb{c}")
            nc.sync.dma_start(z_sb[:], z_rows[:, :, c * Z_COLS : (c + 1) * Z_COLS])
            z_tiles.append(z_sb)
        offsets = held.tile([P, D * V // 16], U16)
        nc.sync.dma_start(offsets[:], offs)
        u_tiles = []
        for d, u in enumerate((u0, u1, u2)):
            u_sb = held.tile([P, V], F32, name=f"u_sb{d}")
            nc.gpsimd.dma_start(u_sb[:], u)
            u_tiles.append(u_sb)
        w_sb = held.tile([P, M], BF16)
        nc.sync.dma_start(w_sb[:], w)
        b_sb = held.tile([P, MB], F32)
        nc.sync.dma_start(b_sb[:], b.rearrange("(p c) o -> p (c o)", c=MB))

        table = held.tile([P, S], F32)
        for t in range(S // T_COLS):
            z_sb = z_tiles[t * T_COLS // Z_COLS]
            first = t * T_COLS % Z_COLS
            projected = psum.tile([P, T_COLS], F32, name="bank")
            for h in range(KH):
                nc.tensor.matmul(
                    projected[:], wt_sb[:, h, :], z_sb[:, h, first : first + T_COLS], start=h == 0, stop=h == KH - 1
                )
            columns = table[:, t * T_COLS : (t + 1) * T_COLS]
            if t % 2 == 0:
                nc.scalar.copy(columns, projected[:])
            else:
                nc.vector.tensor_copy(columns, projected[:])

        w_blocks = w_sb[:].rearrange("r (p c) -> r c p", c=MB)
        out_rows = out.rearrange("(p c) j -> p c j", c=MB)

        def look_up(first, d):
            product = work.tile([P, X_COLS], F32, name=f"product{d}")
            entry = d * V + first
            looked_up = table[:].indirect(offsets[:, entry // 16 : (entry + X_COLS) // 16])
            nc.vector.tensor_tensor(product[:], looked_up, u_tiles[d][:, first : first + X_COLS], MULT)
            return product

        def add(a, b, dtype, name):
            total = work.tile([P, X_COLS], dtype, name=name)
            nc.vector.tensor_tensor(total[:], a[:], b[:], ADD)
            return total

        def dense_layer(first, x_sb, vector_is_free):
            for c in range(MB):
                layer = psum.tile([P, X_COLS], F32, name="bank")
                nc.tensor.matmul(layer[:], w_blocks[:, c, :], x_sb[:], start=True, stop=True)
                y_sb = work.tile([P, X_COLS], F32, name=f"y_sb{c}")
                if c % 2 == 0 or not vector_is_free:
                    nc.scalar.activation(y_sb[:], layer[:], RELU, bias=b_sb[:, c : c + 1])
                else:
                    nc.vector.tensor_scalar(y_sb[:], layer[:], b_sb[:, c : c + 1], 0.0, ADD, MAX)
                nc.sync.dma_start(out_rows[:, c, first : first + X_COLS], y_sb[:])

        left0, left1, left2 = look_up(0, 0), look_up(0, 1), look_up(0, 2)
        left01 = add(left0, left1, F32, "partial")
        right0 = look_up(X_COLS, 0)
        dense_layer(0, add(left01, left2, BF16, "x_sb"), vector_is_free=False)
        right1, right2 = look_up(X_COLS, 1), look_up(X_COLS, 2)
        right01 = add(right0, right1, F32, "partial")
        dense_layer(X_COLS, add(right01, right2, BF16, "x_sb"), vector_is_free=True)
